import numpy as np
import ml_dtypes


def mxq(x, axis, fmt="e4m3"):
    dtype, down = {"e4m3": (ml_dtypes.float8_e4m3fn, 7), "e5m2": (ml_dtypes.float8_e5m2, 14)}[fmt]
    v = np.moveaxis(np.asarray(x, np.float32).astype(ml_dtypes.bfloat16).astype(np.float64), axis, -1)
    blocks = v.reshape(v.shape[:-1] + (-1, 32))
    amax = np.abs(blocks).max(-1, keepdims=True)
    byte = np.maximum(np.where(amax > 0, np.frexp(amax)[1] - 1 + 127, 0) - down, 1)
    scale = np.exp2(byte - 127.0)
    codes = (blocks / scale).astype(np.float32).astype(dtype).astype(np.float64)
    return np.moveaxis((codes * scale).reshape(v.shape), -1, axis)


WIDE = False


def mx_kscale(k):
    if not WIDE:
        return np.ones(k)
    levels = np.array([10, -10, 5, -5, 0])
    if k % 512:
        return np.exp2(np.random.permutation(np.resize(levels, k // 32))).repeat(32)
    a = np.empty((k // 512, 16))
    for p in range(k // 512):
        a[p, :8] = np.random.permutation(np.resize(levels, 8))
        for g in range(8):
            far = levels[np.abs(levels - a[p, g]) >= 10]
            a[p, g + 8] = far[np.random.randint(len(far))]
    return np.exp2(a.ravel()).repeat(32)


BF16 = ml_dtypes.bfloat16


def bf(x):
    return np.asarray(x, np.float32).astype(BF16)


def f64(x):
    return np.asarray(x).astype(np.float64)


E2M1 = np.array([0.0, 0.5, 1.0, 1.5, 2.0, 3.0, 4.0, 6.0, -0.0, -0.5, -1.0, -1.5, -2.0, -3.0, -4.0, -6.0])


def pack_weight(w, fmt):
    k, n = w.shape
    w = f64(bf(w)).reshape(k // 32, 32, n)
    amax = np.abs(w).max(1)
    if fmt == "e4m3":
        byte = np.frexp(amax)[1] - 1 + 127 - 7
    else:
        mant, ex = np.frexp(amax / 6.0)
        byte = np.where(mant > 0.5, ex, ex - 1) + 127
    byte = np.clip(np.where(amax > 0, byte, 1), 1, 254)
    scaled = (w * np.exp2(127.0 - byte)[:, None, :]).reshape(k, n).astype(np.float32)
    by_word = np.ascontiguousarray(scaled.reshape(k // 512, 128, 4, n).transpose(0, 1, 3, 2))
    if fmt == "e4m3":
        words = by_word.astype(ml_dtypes.float8_e4m3fn).view(np.uint8)
    else:
        c = by_word.astype(ml_dtypes.float4_e2m1fn).view(np.uint8) & 0xF
        words = c[..., 0::2] | (c[..., 1::2] << 4)
    return np.ascontiguousarray(words), np.ascontiguousarray(byte.astype(np.uint8).reshape(k // 512, 16, n))


def unpack_weight(words, scales, fmt):
    g, p, n, _ = words.shape
    if fmt == "e4m3":
        vals = np.ascontiguousarray(words).view(ml_dtypes.float8_e4m3fn).astype(np.float64)
    else:
        nib = np.empty((g, p, n, 4), np.uint8)
        nib[..., 0::2] = words & 0xF
        nib[..., 1::2] = words >> 4
        vals = E2M1[nib]
    vals = vals * np.repeat(np.exp2(scales.astype(np.float64) - 127.0), 8, axis=1)[..., None]
    return vals.transpose(0, 1, 3, 2).reshape(g * 512, n)
def pack4(w):
    words, scales = pack_weight(w, "e2m1")
    return words.reshape(words.shape[0], 128, -1), scales


def unpack4(words, scales):
    return unpack_weight(words.reshape(words.shape[0], 128, -1, 2), scales, "e2m1")


E4M3FN = np.array([(-1.0 if i & 128 else 1.0) * ((1.0 + (i & 7) / 8.0) * 2.0 ** (((i >> 3) & 15) - 7) if i & 120 else (i & 7) * 2.0 ** -9) for i in range(256)])


def e4m3fn_bytes(y):
    return np.clip(np.asarray(y, np.float64), -448.0, 448.0).astype(np.float32).astype(ml_dtypes.float8_e4m3fn).view(np.uint8)


def e4m3fn_values(b):
    return E4M3FN[b]


M, K, N, R, G = 2048, 1536, 1024, 512, 128


def setup_inputs():
    s = mx_kscale(K)
    u = mx_kscale(M)
    x = np.random.standard_normal((M, K)) * s
    scale = (np.abs(x).reshape(M, K // G, G).max(axis=2) / 448.0).astype(np.float32)
    v = np.random.standard_normal((M, R)) / np.sqrt(M) / u[:, None]
    v_words, v_scales = pack4(v)
    return {"X_bytes": e4m3fn_bytes(x / np.repeat(f64(scale), G, axis=1)),
            "X_scale": scale,
            "w": bf(np.random.standard_normal((K, N)) / np.sqrt(K) / s[:, None]),
            "gain": bf((1 + 0.1 * np.random.standard_normal(M)) * u),
            "v_words": v_words,
            "v_scales": v_scales,
            "bias": bf(0.3 * np.random.standard_normal(R))}


def reference(X_bytes, X_scale, w, gain, v_words, v_scales, bias):
    x = e4m3fn_values(X_bytes) * np.repeat(f64(X_scale), G, axis=1)
    c = mxq(x, 1, "e4m3") @ mxq(f64(w), 0, "e4m3")
    h = np.abs(c) * f64(gain)[:, None]
    v = unpack4(v_words, v_scales)
    z = mxq(h, 0, "e4m3").T @ v
    return z + f64(bias)[None, :]

@@ -1,0 +1,338 @@
+from contextlib import ExitStack
+
+import concourse.mybir as mybir
+from concourse.masks import make_identity
+
+M, K, N, R = 2048, 1536, 1024, 512
+FLOPS = 2 * M * K * N + 2 * N * M * R
+
+F32 = mybir.dt.float32
+BF16 = mybir.dt.bfloat16
+I32 = mybir.dt.int32
+U32 = mybir.dt.uint32
+U8 = mybir.dt.uint8
+F8 = mybir.dt.float8_e4m3fn
+F8X4 = mybir.dt.float8_e4m3fn_x4
+F4X4 = mybir.dt.float4_e2m1fn_x4
+ALU = mybir.AluOpType
+ACT = mybir.ActivationFunctionType
+
+P = 128
+PASS = 512
+KP = K // PASS
+GROUPS = M // PASS
+STEPS = 2 * GROUPS
+HALF = 512
+QUART = 256
+
+
+def tile_seismic_filter_stack_d4_kernel(tc, X_bytes, X_scale, w, gain, v_words, v_scales, bias, out):
+    nc = tc.nc
+    x_rows = X_bytes.rearrange("(g p t) k -> g p t k", p=P, t=4)
+    w_rows = w.rearrange("(c p t) n -> c p t n", p=P, t=4)
+
+    with ExitStack() as ctx:
+        one = ctx.enter_context(tc.tile_pool(name="one", bufs=1))
+        ring = ctx.enter_context(tc.tile_pool(name="ring", bufs=3))
+        psum = ctx.enter_context(tc.psum_pool(name="psum", bufs=8))
+
+        ident = one.tile([P, P], F32, name="ident")
+        make_identity(nc, ident[:])
+        v_sc = one.tile([P, GROUPS, R], U8, name="v_sc", align_bytes=64)
+        nc.gpsimd.memset(v_sc[:].rearrange("p g r -> p (g r)").bitcast(I32), 0)
+
+        xs = one.tile([P, GROUPS, 48], F32, name="xs")
+        nc.sync.dma_start(out=xs[:], in_=X_scale.rearrange("(g p t) c -> p g (t c)", p=P, t=4))
+        xb = {}
+
+        def load_x(s):
+            x_b = one.tile([P, 2, K], U8, name="x_bytes%d" % s)
+            nc.sync.dma_start(out=x_b[:], in_=x_rows[s // 2][:, 2 * (s % 2) : 2 * (s % 2) + 2, :])
+            xb[s] = x_b
+
+        wr = {}
+
+        def load_w(jh, c):
+            w_raw = one.tile([P, 4, HALF], BF16, name="w_raw%d%d" % (jh, c))
+            nc.sync.dma_start(out=w_raw[:], in_=w_rows[c][:, :, jh * HALF : (jh + 1) * HALF])
+            wr[jh, c] = w_raw
+
+        load_x(0)
+        for c in range(KP):
+            load_w(0, c)
+        load_x(1)
+        g_raw = one.tile([P, GROUPS, 4], BF16, name="g_raw")
+        nc.sync.dma_start(out=g_raw[:], in_=gain.rearrange("(g p t) -> p g t", p=P, t=4))
+        for c in range(KP):
+            load_w(1, c)
+        for s in range(2, STEPS):
+            load_x(s)
+        v_w = one.tile([P, GROUPS, 2 * R], U8, name="v_w", align_bytes=64)
+        for g in range(GROUPS):
+            nc.sync.dma_start(out=v_w[:, g, :].bitcast(I32), in_=v_words[g].bitcast(I32))
+        for q in range(4):
+            nc.sync.dma_start(
+                out=v_sc[32 * q : 32 * q + 4, :, :].bitcast(I32),
+                in_=v_scales[:, 4 * q : 4 * q + 4, :].rearrange("g q r -> q g r").bitcast(I32),
+            )
+        b_row = one.tile([P, R], BF16, name="b_row")
+        nc.sync.dma_start(out=b_row[:], in_=bias.partition_broadcast(P))
+
+        gain_f = one.tile([P, GROUPS * 4], F32, name="gain_f")
+        sign_f = one.tile([P, GROUPS * 4], F32, name="sign_f")
+        wq = [one.tile([P, N], U32, name="wq%d" % c, align_bytes=64) for c in range(KP)]
+        wsc = [one.tile([P, N], U8, name="wsc%d" % c, align_bytes=64) for c in range(KP)]
+        xw, by_pairs, xi, xq, xsc, wi, hp, hi, hq, hsc, bank_x, bank_c, bank_z = [{} for i in range(13)]
+
+        def widen(engine, s, c, tt):
+            g, t = s // 2, 2 * (s % 2) + tt
+            if (s, c) not in xw:
+                x_w = ring.tile([P, 2, PASS], BF16, name="x_w", bufs=12)
+                xw[s, c] = x_w
+            by_pairs[s, c, tt] = engine == "v"
+            for q in range(4):
+                k0 = c * PASS + q * P
+                src = xb[s][:, tt, k0 : k0 + P].bitcast(F8)
+                scale = xs[:, g, t * 12 + c * 4 + q : t * 12 + c * 4 + q + 1]
+                if engine == "v":
+                    dst = xw[s, c][:, tt, :].rearrange("p (u k e) -> p k u e", u=2, e=2)[:, 32 * q : 32 * q + 32, :, :]
+                    nc.vector.tensor_scalar(
+                        out=dst, in0=src.rearrange("p (k u e) -> p k u e", u=2, e=2), scalar1=scale, scalar2=None, op0=ALU.mult
+                    )
+                else:
+                    nc.scalar.activation(out=xw[s, c][:, tt, q * P : q * P + P], in_=src, func=ACT.Copy, scale=scale)
+
+        def turn(engine, s, c):
+            bank = psum.tile([P, 512], F32, name="bank")
+            for tt in range(2):
+                words = xw[s, c][:, tt, :].bitcast(F32)
+                for u in range(2):
+                    pick = words[:, u * P : u * P + P] if by_pairs[s, c, tt] else words[:, u : 2 * P : 2]
+                    j = 2 * tt + u
+                    nc.tensor.transpose(bank[:, j * P : j * P + P], pick, ident[:])
+            bank_x[s, c] = bank
+
+        def collect(engine, s, c):
+            x_i = ring.tile([P, 2 * P * 4], BF16, name="x_i", align_bytes=64, bufs=6)
+            dst = x_i[:].bitcast(F32).rearrange("p (a m u) -> p a m u", a=2, u=2)
+            src = bank_x[s, c][:].rearrange("p (a u m) -> p a m u", a=2, u=2)
+            if engine == "v":
+                nc.vector.tensor_copy(out=dst, in_=src)
+            else:
+                nc.scalar.copy(out=dst, in_=src)
+            xi[s, c] = x_i
+
+        def quant_x(engine, s, c):
+            codes = one.tile([P, 2 * P], U32, name="xq%d%d" % (s, c), align_bytes=64)
+            scales = one.tile([P, 2 * P], U8, name="xsc%d%d" % (s, c), align_bytes=64)
+            nc.vector.quantize_mx(out=codes[:].bitcast(F8X4), scales=scales[:], in_=xi[s, c][:])
+            xq[s, c], xsc[s, c] = codes, scales
+
+        def weave_w(engine, c, q):
+            w_i = ring.tile([P, QUART * 4], BF16, name="w_i", align_bytes=64, bufs=6)
+            cols = slice(q % 2 * QUART, q % 2 * QUART + QUART)
+            dst = w_i[:].rearrange("p (n t) -> p n t", t=4)
+            src = wr[q // 2, c][:, :, cols].rearrange("p t n -> p n t")
+            if engine == "v":
+                nc.vector.tensor_copy(out=dst, in_=src)
+            else:
+                nc.scalar.copy(out=dst, in_=src)
+            wi[c, q] = w_i
+
+        def quant_w(engine, c, q):
+            cols = slice(q * QUART, q * QUART + QUART)
+            nc.vector.quantize_mx(out=wq[c][:, cols].bitcast(F8X4), scales=wsc[c][:, cols], in_=wi[c, q][:])
+
+        def signs(engine):
+            nc.vector.tensor_copy(out=gain_f[:], in_=g_raw[:].rearrange("p g t -> p (g t)"))
+            nc.vector.tensor_scalar(out=sign_f[:], in0=gain_f[:], scalar1=0.0, scalar2=2.0, op0=ALU.is_ge, op1=ALU.mult)
+            nc.vector.tensor_scalar(out=sign_f[:], in0=sign_f[:], scalar1=-1.0, scalar2=None, op0=ALU.add)
+
+        def correlate(engine, s, tt, n0, width):
+            jh = n0 // HALF
+            if n0 % HALF == 0:
+                bank = psum.tile([P, 512], F32, name="bank")
+                bank_c[s, tt, jh] = bank
+            rows = slice(tt * P, tt * P + P)
+            cols = slice(n0, n0 + width)
+            for c in range(KP):
+                nc.tensor.matmul_mx(
+                    out=bank_c[s, tt, jh][:, n0 % HALF : n0 % HALF + width],
+                    lhsT=xq[s, c][:, rows].bitcast(F8X4),
+                    lhsT_scale=xsc[s, c][:, rows],
+                    rhs=wq[c][:, cols].bitcast(F8X4),
+                    rhs_scale=wsc[c][:, cols],
+                    start=(c == 0),
+                    stop=(c == KP - 1),
+                )
+
+        def rectify(engine, s, tt, jh):
+            g, t = s // 2, 2 * (s % 2) + tt
+            if (g, jh) not in hp:
+                h_p = ring.tile([P, 4, HALF], BF16, name="h_p", bufs=4)
+                hp[g, jh] = h_p
+            nc.scalar.activation(
+                out=hp[g, jh][:, t, :], in_=bank_c[s, tt, jh][:], func=ACT.Abs, scale=gain_f[:, 4 * g + t : 4 * g + t + 1]
+            )
+
+        def resign(engine, s, tt, jh):
+            g, t = s // 2, 2 * (s % 2) + tt
+            h = hp[g, jh][:, t, :]
+            nc.vector.tensor_scalar(out=h, in0=h, scalar1=sign_f[:, 4 * g + t : 4 * g + t + 1], scalar2=None, op0=ALU.mult)
+
+        def weave_h(engine, g, jh):
+            h_i = ring.tile([P, HALF * 4], BF16, name="h_i", align_bytes=64)
+            nc.vector.tensor_copy(out=h_i[:].rearrange("p (n t) -> p n t", t=4), in_=hp[g, jh][:].rearrange("p t n -> p n t"))
+            hi[g, jh] = h_i
+
+        def quant_h(engine, g, jh):
+            codes = one.tile([P, HALF], U32, name="hq%d%d" % (g, jh), align_bytes=64)
+            scales = one.tile([P, HALF], U8, name="hsc%d%d" % (g, jh), align_bytes=64)
+            nc.vector.quantize_mx(out=codes[:].bitcast(F8X4), scales=scales[:], in_=hi[g, jh][:])
+            hq[g, jh], hsc[g, jh] = codes, scales
+
+        def stack(engine, j, g):
+            if g == 0:
+                bank = psum.tile([P, 512], F32, name="bank")
+                bank_z[j] = bank
+            cols = slice(j % 4 * P, j % 4 * P + P)
+            nc.tensor.matmul_mx(
+                out=bank_z[j][:],
+                lhsT=hq[g, j // 4][:, cols].bitcast(F8X4),
+                lhsT_scale=hsc[g, j // 4][:, cols],
+                rhs=v_w[:, g, :].bitcast(F4X4),
+                rhs_scale=v_sc[:, g, :],
+                start=(g == 0),
+                stop=(g == GROUPS - 1),
+            )
+
+        def finish(engine, j):
+            z = ring.tile([P, R], F32, name="z", bufs=4)
+            nc.vector.tensor_tensor(out=z[:], in0=bank_z[j][:], in1=b_row[:], op=ALU.add)
+            nc.sync.dma_start(out=out[j * P : j * P + P, :], in_=z[:])
+
+        def needs(fn, k):
+            if fn == turn:
+                return [(widen, k[0], k[1], tt) for tt in range(2)]
+            if fn == collect:
+                return [(turn, k[0], k[1])]
+            if fn == quant_x:
+                return [(collect, k[0], k[1])]
+            if fn == quant_w:
+                return [(weave_w, k[0], k[1])]
+            if fn == correlate:
+                qs = range(k[2] // QUART, (k[2] + k[3]) // QUART)
+                return [(quant_x, k[0], c) for c in range(KP)] + [(quant_w, c, q) for c in range(KP) for q in qs]
+            if fn == rectify:
+                return [(signs,)]
+            if fn == resign:
+                return [(rectify, k[0], k[1], k[2])]
+            if fn == weave_h:
+                return [(resign, s, tt, k[1]) for s in (2 * k[0], 2 * k[0] + 1) for tt in range(2)]
+            if fn == quant_h:
+                return [(weave_h, k[0], k[1])]
+            if fn == stack:
+                return [(quant_h, k[1], k[0] // 4)]
+            if fn == finish:
+                return [(stack, k[0], GROUPS - 1)]
+            return []
+
+        def quarters(s, tt, jh):
+            return [(correlate, s, tt, jh * HALF + i * QUART, QUART) for i in range(2)]
+
+        pe, v, sc = [], [], []
+        v += [(widen, 0, 2, 0), (widen, 0, 2, 1)]
+        sc += [(widen, 0, 0, 0), (widen, 0, 0, 1), (widen, 0, 1, 0), (widen, 0, 1, 1)]
+        pe += [(turn, 0, 2), (turn, 0, 0), (turn, 0, 1)]
+        sc += [(collect, 0, 2), (collect, 0, 0), (collect, 0, 1)]
+        v += [(weave_w, 0, 0), (weave_w, 0, 1), (quant_w, 0, 0), (weave_w, 1, 0), (quant_w, 0, 1), (weave_w, 1, 1), (quant_w, 1, 0)]
+        v += [(weave_w, 2, 0), (quant_w, 1, 1), (quant_x, 0, 2), (quant_w, 2, 0), (quant_x, 0, 0), (weave_w, 2, 1), (quant_x, 0, 1), (quant_w, 2, 1)]
+        pe += [(correlate, 0, tt, 0, QUART) for tt in range(2)]
+        pe += [(correlate, 0, tt, QUART, QUART) for tt in range(2)]
+        sc += [(widen, 1, c, tt) for c in range(2) for tt in range(2)]
+        v += [(signs,), (widen, 1, 2, 0), (widen, 1, 2, 1)]
+        pe += [(turn, 1, 0), (turn, 1, 1), (turn, 1, 2)]
+        sc += [(collect, 1, c) for c in range(3)]
+        v += [(weave_w, 0, 2), (weave_w, 0, 3), (quant_w, 0, 2), (weave_w, 1, 2), (quant_x, 1, 0), (quant_w, 0, 3), (weave_w, 1, 3), (quant_x, 1, 1), (quant_w, 1, 2)]
+        v += [(weave_w, 2, 2), (quant_x, 1, 2), (quant_w, 1, 3), (weave_w, 2, 3), (quant_w, 2, 2), (widen, 2, 2, 0), (quant_w, 2, 3), (widen, 2, 2, 1)]
+        pe += [(correlate, 1, tt, 0, HALF) for tt in range(2)]
+        sc += [(rectify, 0, tt, 0) for tt in range(2)] + [(widen, 2, c, tt) for c in range(2) for tt in range(2)] + [(rectify, 1, tt, 0) for tt in range(2)]
+        pe += [(turn, 2, c) for c in range(3)]
+        pe += [(correlate, s, tt, HALF, HALF) for s in range(2) for tt in range(2)]
+        sc += [(collect, 2, 0), (collect, 2, 2)]
+        v += [(collect, 2, 1), (quant_x, 2, 0), (quant_x, 2, 1), (quant_x, 2, 2)]
+        sc += [(rectify, s, tt, 1) for s in range(2) for tt in range(2)]
+        v += [(resign, s, tt, 0) for s in range(2) for tt in range(2)]
+        v += [(widen, 3, 2, 0), (widen, 3, 2, 1)]
+        v += [(weave_h, 0, 0)]
+        sc += [(widen, 3, c, tt) for c in range(2) for tt in range(2)]
+        v += [(resign, s, tt, 1) for s in range(2) for tt in range(2)]
+        v += [(quant_h, 0, 0)]
+        for s in range(2, STEPS):
+            last = s == STEPS - 1
+            g = s // 2
+            pe += [(correlate, s, tt, 0, HALF) for tt in range(2)]
+            if not last:
+                pe += [(turn, s + 1, c) for c in range(3)]
+            else:
+                pe += [(stack, j, gg) for j in range(4) for gg in range(3)]
+            pe += [(correlate, s, tt, HALF, HALF) for tt in range(2)]
+            nw = s + 2 < STEPS
+            if s % 2 == 0:
+                v += [(weave_h, g - 1, 1)]
+            else:
+                v += [(resign, s - 1, 0, 1), (resign, s - 1, 1, 1)]
+            sc += [(rectify, s, 0, 0)]
+            if not last:
+                sc += [(collect, s + 1, 0)]
+                v += [(collect, s + 1, 1)]
+                sc += [(rectify, s, 1, 0)]
+                sc += [(collect, s + 1, 2)]
+                v += [(quant_x, s + 1, 0)]
+            else:
+                sc += [(rectify, s, 1, 0)]
+            if s % 2 == 0:
+                v += [(quant_h, g - 1, 1)]
+            if not last:
+                v += [(quant_x, s + 1, 1), (quant_x, s + 1, 2)]
+            v += [(resign, s, 0, 0), (resign, s, 1, 0)]
+            if nw:
+                v += [(widen, s + 2, 2, 0), (widen, s + 2, 2, 1)]
+                if s % 2:
+                    v += [(widen, s + 2, 1, 0), (widen, s + 2, 1, 1)]
+                else:
+                    sc += [(widen, s + 2, 1, 0), (widen, s + 2, 1, 1)]
+                sc += [(widen, s + 2, 0, 0), (widen, s + 2, 0, 1)]
+            sc += [(rectify, s, 0, 1), (rectify, s, 1, 1)]
+            if s % 2:
+                v += [(weave_h, g, 0), (resign, s, 0, 1), (resign, s, 1, 1), (quant_h, g, 0)]
+        v += [(weave_h, 3, 1)]
+        pe += [(stack, j, 3) for j in range(4)]
+        v += [(finish, 0), (quant_h, 3, 1), (finish, 1), (finish, 2), (finish, 3)]
+        pe += [(stack, j, g) for j in range(4, 8) for g in range(3)]
+        pe += [(stack, j, 3) for j in range(4, 8)]
+        v += [(finish, j) for j in range(4, 8)]
+        queues = {"p": pe, "v": v, "s": sc}
+        at = {"p": 0, "v": 0, "s": 0}
+        issued = set()
+        halves = {}
+        while any(at[e] < len(queues[e]) for e in queues):
+            moved = False
+            for e in queues:
+                while at[e] < len(queues[e]):
+                    fn, key = queues[e][at[e]][0], queues[e][at[e]][1:]
+                    need = needs(fn, key)
+                    if fn == rectify:
+                        need = need + [("corr",) + key]
+                    if any(n not in issued for n in need):
+                        break
+                    fn(e, *key)
+                    issued.add((fn,) + key)
+                    if fn == correlate:
+                        w = halves.get((key[0], key[1], key[2] // HALF), 0) + key[3]
+                        halves[key[0], key[1], key[2] // HALF] = w
+                        if w == HALF:
+                            issued.add(("corr", key[0], key[1], key[2] // HALF))
+                    at[e] += 1
+                    moved = True
+            assert moved

@@ -35,6 +35,7 @@ def tile_seismic_filter_stack_d4_kernel(tc, X_bytes, X_scale, w, gain, v_words, 
         one = ctx.enter_context(tc.tile_pool(name="one", bufs=1))
         ring = ctx.enter_context(tc.tile_pool(name="ring", bufs=3))
         psum = ctx.enter_context(tc.psum_pool(name="psum", bufs=8))
+        ctx.enter_context(tc.manual_schedule())
 
         ident = one.tile([P, P], F32, name="ident")
         make_identity(nc, ident[:])
@@ -241,77 +242,64 @@ def tile_seismic_filter_stack_d4_kernel(tc, X_bytes, X_scale, w, gain, v_words, 
             return [(correlate, s, tt, jh * HALF + i * QUART, QUART) for i in range(2)]
 
         pe, v, sc = [], [], []
-        v += [(widen, 0, 2, 0), (widen, 0, 2, 1)]
-        sc += [(widen, 0, 0, 0), (widen, 0, 0, 1), (widen, 0, 1, 0), (widen, 0, 1, 1)]
-        pe += [(turn, 0, 2), (turn, 0, 0), (turn, 0, 1)]
-        sc += [(collect, 0, 2), (collect, 0, 0), (collect, 0, 1)]
-        v += [(weave_w, 0, 0), (weave_w, 0, 1), (quant_w, 0, 0), (weave_w, 1, 0), (quant_w, 0, 1), (weave_w, 1, 1), (quant_w, 1, 0)]
-        v += [(weave_w, 2, 0), (quant_w, 1, 1), (quant_x, 0, 2), (quant_w, 2, 0), (quant_x, 0, 0), (weave_w, 2, 1), (quant_x, 0, 1), (quant_w, 2, 1)]
-        pe += [(correlate, 0, tt, 0, QUART) for tt in range(2)]
-        pe += [(correlate, 0, tt, QUART, QUART) for tt in range(2)]
-        sc += [(widen, 1, c, tt) for c in range(2) for tt in range(2)]
-        v += [(signs,), (widen, 1, 2, 0), (widen, 1, 2, 1)]
-        pe += [(turn, 1, 0), (turn, 1, 1), (turn, 1, 2)]
-        sc += [(collect, 1, c) for c in range(3)]
-        v += [(weave_w, 0, 2), (weave_w, 0, 3), (quant_w, 0, 2), (weave_w, 1, 2), (quant_x, 1, 0), (quant_w, 0, 3), (weave_w, 1, 3), (quant_x, 1, 1), (quant_w, 1, 2)]
-        v += [(weave_w, 2, 2), (quant_x, 1, 2), (quant_w, 1, 3), (weave_w, 2, 3), (quant_w, 2, 2), (widen, 2, 2, 0), (quant_w, 2, 3), (widen, 2, 2, 1)]
-        pe += [(correlate, 1, tt, 0, HALF) for tt in range(2)]
-        sc += [(rectify, 0, tt, 0) for tt in range(2)] + [(widen, 2, c, tt) for c in range(2) for tt in range(2)] + [(rectify, 1, tt, 0) for tt in range(2)]
-        pe += [(turn, 2, c) for c in range(3)]
-        pe += [(correlate, s, tt, HALF, HALF) for s in range(2) for tt in range(2)]
-        sc += [(collect, 2, 0), (collect, 2, 2)]
-        v += [(collect, 2, 1), (quant_x, 2, 0), (quant_x, 2, 1), (quant_x, 2, 2)]
-        sc += [(rectify, s, tt, 1) for s in range(2) for tt in range(2)]
-        v += [(resign, s, tt, 0) for s in range(2) for tt in range(2)]
-        v += [(widen, 3, 2, 0), (widen, 3, 2, 1)]
-        v += [(weave_h, 0, 0)]
-        sc += [(widen, 3, c, tt) for c in range(2) for tt in range(2)]
-        v += [(resign, s, tt, 1) for s in range(2) for tt in range(2)]
-        v += [(quant_h, 0, 0)]
-        for s in range(2, STEPS):
-            last = s == STEPS - 1
-            g = s // 2
-            pe += [(correlate, s, tt, 0, HALF) for tt in range(2)]
-            if not last:
-                pe += [(turn, s + 1, c) for c in range(3)]
-            else:
-                pe += [(stack, j, gg) for j in range(4) for gg in range(3)]
-            pe += [(correlate, s, tt, HALF, HALF) for tt in range(2)]
-            nw = s + 2 < STEPS
-            if s % 2 == 0:
-                v += [(weave_h, g - 1, 1)]
-            else:
-                v += [(resign, s - 1, 0, 1), (resign, s - 1, 1, 1)]
-            sc += [(rectify, s, 0, 0)]
-            if not last:
-                sc += [(collect, s + 1, 0)]
-                v += [(collect, s + 1, 1)]
-                sc += [(rectify, s, 1, 0)]
-                sc += [(collect, s + 1, 2)]
-                v += [(quant_x, s + 1, 0)]
-            else:
-                sc += [(rectify, s, 1, 0)]
-            if s % 2 == 0:
-                v += [(quant_h, g - 1, 1)]
-            if not last:
-                v += [(quant_x, s + 1, 1), (quant_x, s + 1, 2)]
-            v += [(resign, s, 0, 0), (resign, s, 1, 0)]
-            if nw:
-                v += [(widen, s + 2, 2, 0), (widen, s + 2, 2, 1)]
-                if s % 2:
-                    v += [(widen, s + 2, 1, 0), (widen, s + 2, 1, 1)]
-                else:
-                    sc += [(widen, s + 2, 1, 0), (widen, s + 2, 1, 1)]
-                sc += [(widen, s + 2, 0, 0), (widen, s + 2, 0, 1)]
-            sc += [(rectify, s, 0, 1), (rectify, s, 1, 1)]
-            if s % 2:
-                v += [(weave_h, g, 0), (resign, s, 0, 1), (resign, s, 1, 1), (quant_h, g, 0)]
-        v += [(weave_h, 3, 1)]
-        pe += [(stack, j, 3) for j in range(4)]
-        v += [(finish, 0), (quant_h, 3, 1), (finish, 1), (finish, 2), (finish, 3)]
-        pe += [(stack, j, g) for j in range(4, 8) for g in range(3)]
-        pe += [(stack, j, 3) for j in range(4, 8)]
-        v += [(finish, j) for j in range(4, 8)]
+        pe += [
+            (turn, 0, 0), (turn, 0, 2), (turn, 0, 1), (turn, 1, 0), (turn, 1, 1), (turn, 1, 2),
+            (correlate, 0, 0, 0, QUART), (correlate, 0, 1, 0, QUART), (correlate, 0, 0, 256, QUART), (correlate, 0, 1, 256, QUART), (correlate, 1, 0, 0, QUART), (correlate, 1, 1, 0, QUART),
+            (correlate, 1, 0, 256, QUART), (correlate, 1, 1, 256, QUART), (correlate, 0, 0, 512, QUART), (correlate, 0, 1, 512, QUART), (correlate, 1, 0, 512, QUART), (correlate, 1, 1, 512, QUART),
+            (turn, 2, 0), (turn, 2, 1), (turn, 2, 2), (correlate, 0, 0, 768, QUART), (correlate, 0, 1, 768, QUART), (correlate, 1, 0, 768, QUART),
+            (correlate, 1, 1, 768, QUART), (turn, 3, 0), (turn, 3, 1), (turn, 3, 2), (correlate, 2, 0, 0, HALF), (correlate, 2, 1, 0, HALF),
+            (correlate, 2, 0, 512, HALF), (correlate, 2, 1, 512, HALF), (turn, 4, 0), (turn, 4, 1), (turn, 4, 2), (correlate, 3, 0, 0, HALF),
+            (correlate, 3, 1, 0, HALF), (correlate, 3, 0, 512, HALF), (correlate, 3, 1, 512, HALF), (turn, 5, 0), (turn, 5, 1), (turn, 5, 2),
+            (correlate, 4, 0, 0, HALF), (correlate, 4, 1, 0, HALF), (correlate, 4, 0, 512, HALF), (correlate, 4, 1, 512, HALF), (turn, 6, 0), (turn, 6, 1),
+            (turn, 6, 2), (correlate, 5, 0, 0, HALF), (correlate, 5, 1, 0, HALF), (correlate, 5, 0, 512, HALF), (correlate, 5, 1, 512, HALF), (turn, 7, 0),
+            (turn, 7, 1), (turn, 7, 2), (correlate, 6, 0, 0, HALF), (correlate, 6, 1, 0, HALF), (correlate, 6, 0, 512, HALF), (correlate, 6, 1, 512, HALF),
+            (correlate, 7, 0, 0, HALF), (correlate, 7, 1, 0, HALF), (correlate, 7, 0, 512, HALF), (correlate, 7, 1, 512, HALF), (stack, 0, 0), (stack, 1, 0),
+            (stack, 2, 0), (stack, 3, 0), (stack, 0, 1), (stack, 1, 1), (stack, 2, 1), (stack, 3, 1),
+            (stack, 0, 2), (stack, 1, 2), (stack, 2, 2), (stack, 3, 2), (stack, 0, 3), (stack, 1, 3),
+            (stack, 2, 3), (stack, 3, 3), (stack, 4, 0), (stack, 5, 0), (stack, 6, 0), (stack, 7, 0),
+            (stack, 4, 1), (stack, 5, 1), (stack, 6, 1), (stack, 7, 1), (stack, 4, 2), (stack, 5, 2),
+            (stack, 6, 2), (stack, 7, 2), (stack, 4, 3), (stack, 5, 3), (stack, 6, 3), (stack, 7, 3),
+        ]
+        v += [
+            (widen, 0, 0, 0), (widen, 0, 2, 0), (widen, 0, 1, 0), (widen, 0, 1, 1), (weave_w, 0, 0), (weave_w, 1, 0),
+            (weave_w, 0, 1), (weave_w, 2, 0), (quant_w, 0, 0), (widen, 1, 0, 1), (widen, 1, 2, 1), (quant_w, 1, 0),
+            (weave_w, 2, 1), (quant_w, 0, 1), (signs,), (quant_w, 2, 0), (quant_x, 0, 0), (quant_x, 0, 2),
+            (quant_x, 0, 1), (quant_w, 1, 1), (quant_w, 2, 1), (weave_w, 0, 2), (quant_x, 1, 0), (quant_x, 1, 1),
+            (quant_x, 1, 2), (weave_w, 2, 2), (quant_w, 0, 2), (quant_w, 1, 2), (weave_w, 1, 3), (quant_w, 2, 2),
+            (weave_w, 2, 3), (quant_w, 0, 3), (resign, 0, 0, 0), (widen, 2, 0, 1), (widen, 2, 1, 0), (widen, 2, 1, 1),
+            (quant_w, 1, 3), (resign, 0, 1, 0), (quant_w, 2, 3), (resign, 1, 0, 0), (widen, 3, 0, 1), (widen, 3, 1, 0),
+            (widen, 3, 1, 1), (widen, 3, 2, 0), (widen, 3, 2, 1), (resign, 1, 1, 0), (quant_x, 2, 0), (quant_x, 2, 1),
+            (quant_x, 2, 2), (weave_h, 0, 0), (widen, 4, 0, 0), (widen, 4, 0, 1), (quant_h, 0, 0), (widen, 4, 1, 0),
+            (widen, 4, 2, 0), (resign, 0, 0, 1), (quant_x, 3, 0), (quant_x, 3, 1), (quant_x, 3, 2), (resign, 0, 1, 1),
+            (widen, 5, 0, 0), (widen, 5, 0, 1), (resign, 1, 0, 1), (widen, 5, 1, 1), (widen, 5, 2, 0), (widen, 5, 2, 1),
+            (resign, 1, 1, 1), (resign, 2, 0, 0), (quant_x, 4, 0), (quant_x, 4, 1), (quant_x, 4, 2), (weave_h, 0, 1),
+            (resign, 2, 1, 0), (widen, 6, 0, 0), (widen, 6, 0, 1), (widen, 6, 1, 0), (widen, 6, 1, 1), (quant_h, 0, 1),
+            (widen, 6, 2, 0), (resign, 2, 0, 1), (resign, 2, 1, 1), (resign, 3, 0, 0), (quant_x, 5, 0), (quant_x, 5, 1),
+            (quant_x, 5, 2), (resign, 3, 1, 0), (widen, 7, 0, 0), (widen, 7, 1, 1), (widen, 7, 2, 0), (widen, 7, 2, 1),
+            (resign, 3, 0, 1), (weave_h, 1, 0), (resign, 3, 1, 1), (resign, 4, 0, 0), (quant_x, 6, 0), (quant_x, 6, 1),
+            (quant_x, 6, 2), (quant_h, 1, 0), (weave_h, 1, 1), (resign, 4, 1, 0), (resign, 4, 0, 1), (quant_h, 1, 1),
+            (resign, 4, 1, 1), (resign, 5, 0, 0), (quant_x, 7, 0), (quant_x, 7, 1), (quant_x, 7, 2), (resign, 5, 1, 0),
+            (resign, 5, 0, 1), (weave_h, 2, 0), (resign, 5, 1, 1), (resign, 6, 0, 0), (quant_h, 2, 0), (weave_h, 2, 1),
+            (resign, 6, 1, 0), (resign, 6, 0, 1), (quant_h, 2, 1), (resign, 6, 1, 1), (resign, 7, 0, 0), (resign, 7, 1, 0),
+            (resign, 7, 0, 1), (weave_h, 3, 0), (resign, 7, 1, 1), (quant_h, 3, 0), (weave_h, 3, 1), (quant_h, 3, 1),
+            (finish, 0), (finish, 1), (finish, 2), (finish, 3), (finish, 4), (finish, 5),
+            (finish, 6), (finish, 7),
+        ]
+        sc += [
+            (widen, 0, 0, 1), (widen, 0, 2, 1), (collect, 0, 0), (collect, 0, 2), (collect, 0, 1), (weave_w, 1, 1),
+            (widen, 1, 0, 0), (widen, 1, 1, 0), (widen, 1, 1, 1), (widen, 1, 2, 0), (collect, 1, 0), (collect, 1, 1),
+            (collect, 1, 2), (weave_w, 1, 2), (rectify, 0, 0, 0), (weave_w, 0, 3), (rectify, 0, 1, 0), (rectify, 1, 0, 0),
+            (widen, 2, 0, 0), (widen, 2, 2, 0), (widen, 2, 2, 1), (rectify, 1, 1, 0), (collect, 2, 0), (collect, 2, 1),
+            (collect, 2, 2), (widen, 3, 0, 0), (rectify, 0, 0, 1), (rectify, 0, 1, 1), (collect, 3, 0), (collect, 3, 1),
+            (collect, 3, 2), (rectify, 1, 0, 1), (widen, 4, 1, 1), (widen, 4, 2, 1), (rectify, 1, 1, 1), (rectify, 2, 0, 0),
+            (collect, 4, 0), (collect, 4, 1), (collect, 4, 2), (rectify, 2, 1, 0), (widen, 5, 1, 0), (rectify, 2, 0, 1),
+            (rectify, 2, 1, 1), (rectify, 3, 0, 0), (collect, 5, 0), (collect, 5, 1), (collect, 5, 2), (rectify, 3, 1, 0),
+            (widen, 6, 2, 1), (rectify, 3, 0, 1), (rectify, 3, 1, 1), (rectify, 4, 0, 0), (collect, 6, 0), (collect, 6, 1),
+            (collect, 6, 2), (rectify, 4, 1, 0), (widen, 7, 0, 1), (widen, 7, 1, 0), (rectify, 4, 0, 1), (rectify, 4, 1, 1),
+            (rectify, 5, 0, 0), (collect, 7, 0), (collect, 7, 1), (collect, 7, 2), (rectify, 5, 1, 0), (rectify, 5, 0, 1),
+            (rectify, 5, 1, 1), (rectify, 6, 0, 0), (rectify, 6, 1, 0), (rectify, 6, 0, 1), (rectify, 6, 1, 1), (rectify, 7, 0, 0),
+            (rectify, 7, 1, 0), (rectify, 7, 0, 1), (rectify, 7, 1, 1),
+        ]
         queues = {"p": pe, "v": v, "s": sc}
         at = {"p": 0, "v": 0, "s": 0}
         issued = set()

@@ -23,6 +23,7 @@ KP = K // PASS
 GROUPS = M // PASS
 STEPS = 2 * GROUPS
 HALF = 512
+X_PARTS = [(0, 512), (512, 1024), (1024, 1536)]
 QUART = 256
 
 
@@ -42,14 +43,23 @@ def tile_seismic_filter_stack_d4_kernel(tc, X_bytes, X_scale, w, gain, v_words, 
         v_sc = one.tile([P, GROUPS, R], U8, name="v_sc", align_bytes=64)
         nc.gpsimd.memset(v_sc[:].rearrange("p g r -> p (g r)").bitcast(I32), 0)
 
+        minus = one.tile([P, 1], F32, name="minus")
+        unit = one.tile([P, 1], F32, name="unit")
+        nc.vector.memset(minus[:], -1.0)
+        nc.scalar.activation(out=unit[:], in_=minus[:], func=ACT.Abs)
+
         xs = one.tile([P, GROUPS, 48], F32, name="xs")
-        nc.sync.dma_start(out=xs[:], in_=X_scale.rearrange("(g p t) c -> p g (t c)", p=P, t=4))
+        x_scale = X_scale.rearrange("(g p t) c -> p g (t c)", p=P, t=4)
+        nc.sync.dma_start(out=xs[:, 0, :], in_=x_scale[:, 0, :])
         xb = {}
 
         def load_x(s):
-            x_b = one.tile([P, 2, K], U8, name="x_bytes%d" % s)
-            nc.sync.dma_start(out=x_b[:], in_=x_rows[s // 2][:, 2 * (s % 2) : 2 * (s % 2) + 2, :])
-            xb[s] = x_b
+            rows = x_rows[s // 2][:, 2 * (s % 2) : 2 * (s % 2) + 2, :]
+            for a, b in X_PARTS if s == 0 else [(0, K)]:
+                x_b = one.tile([P, 2, b - a], U8, name="x_bytes%d_%d" % (s, a))
+                nc.sync.dma_start(out=x_b[:], in_=rows[:, :, a:b])
+                for k in range(a, b, P):
+                    xb[s, k] = x_b[:, :, k - a : k - a + P]
 
         wr = {}
 
@@ -62,6 +72,7 @@ def tile_seismic_filter_stack_d4_kernel(tc, X_bytes, X_scale, w, gain, v_words, 
         for c in range(KP):
             load_w(0, c)
         load_x(1)
+        nc.sync.dma_start(out=xs[:, 1:, :], in_=x_scale[:, 1:, :])
         g_raw = one.tile([P, GROUPS, 4], BF16, name="g_raw")
         nc.sync.dma_start(out=g_raw[:], in_=gain.rearrange("(g p t) -> p g t", p=P, t=4))
         for c in range(KP):
@@ -93,7 +104,7 @@ def tile_seismic_filter_stack_d4_kernel(tc, X_bytes, X_scale, w, gain, v_words, 
             by_pairs[s, c, tt] = engine == "v"
             for q in range(4):
                 k0 = c * PASS + q * P
-                src = xb[s][:, tt, k0 : k0 + P].bitcast(F8)
+                src = xb[s, k0][:, tt, :].bitcast(F8)
                 scale = xs[:, g, t * 12 + c * 4 + q : t * 12 + c * 4 + q + 1]
                 if engine == "v":
                     dst = xw[s, c][:, tt, :].rearrange("p (u k e) -> p k u e", u=2, e=2)[:, 32 * q : 32 * q + 32, :, :]
@@ -132,8 +143,8 @@ def tile_seismic_filter_stack_d4_kernel(tc, X_bytes, X_scale, w, gain, v_words, 
         def weave_w(engine, c, q):
             w_i = ring.tile([P, QUART * 4], BF16, name="w_i", align_bytes=64, bufs=6)
             cols = slice(q % 2 * QUART, q % 2 * QUART + QUART)
-            dst = w_i[:].rearrange("p (n t) -> p n t", t=4)
-            src = wr[q // 2, c][:, :, cols].rearrange("p t n -> p n t")
+            dst = w_i[:].rearrange("p (n i t) -> p n t i", i=4, t=4)
+            src = wr[q // 2, c][:, :, cols].rearrange("p t (n i) -> p n t i", i=4)
             if engine == "v":
                 nc.vector.tensor_copy(out=dst, in_=src)
             else:
@@ -145,9 +156,9 @@ def tile_seismic_filter_stack_d4_kernel(tc, X_bytes, X_scale, w, gain, v_words, 
             nc.vector.quantize_mx(out=wq[c][:, cols].bitcast(F8X4), scales=wsc[c][:, cols], in_=wi[c, q][:])
 
         def signs(engine):
-            nc.vector.tensor_copy(out=gain_f[:], in_=g_raw[:].rearrange("p g t -> p (g t)"))
-            nc.vector.tensor_scalar(out=sign_f[:], in0=gain_f[:], scalar1=0.0, scalar2=2.0, op0=ALU.is_ge, op1=ALU.mult)
-            nc.vector.tensor_scalar(out=sign_f[:], in0=sign_f[:], scalar1=-1.0, scalar2=None, op0=ALU.add)
+            nc.gpsimd.tensor_copy(out=gain_f[:], in_=g_raw[:].rearrange("p g t -> p (g t)"))
+            nc.gpsimd.tensor_scalar(out=sign_f[:], in0=gain_f[:], scalar1=0.0, scalar2=2.0, op0=ALU.is_ge, op1=ALU.mult)
+            nc.gpsimd.tensor_scalar(out=sign_f[:], in0=sign_f[:], scalar1=unit[:], scalar2=None, op0=ALU.subtract)
 
         def correlate(engine, s, tt, n0, width):
             jh = n0 // HALF
@@ -181,16 +192,25 @@ def tile_seismic_filter_stack_d4_kernel(tc, X_bytes, X_scale, w, gain, v_words, 
             h = hp[g, jh][:, t, :]
             nc.vector.tensor_scalar(out=h, in0=h, scalar1=sign_f[:, 4 * g + t : 4 * g + t + 1], scalar2=None, op0=ALU.mult)
 
-        def weave_h(engine, g, jh):
-            h_i = ring.tile([P, HALF * 4], BF16, name="h_i", align_bytes=64)
-            nc.vector.tensor_copy(out=h_i[:].rearrange("p (n t) -> p n t", t=4), in_=hp[g, jh][:].rearrange("p t n -> p n t"))
-            hi[g, jh] = h_i
+        def weave_h(engine, g, jh, n0, width):
+            h_i = ring.tile([P, HALF * 4], BF16, name="h_i", align_bytes=64, bufs=4)
+            dst = h_i[:, : 4 * width].rearrange("p (n i t) -> p n t i", i=4, t=4)
+            src = hp[g, jh][:, :, n0 : n0 + width].rearrange("p t (n i) -> p n t i", i=4)
+            if engine == "v":
+                nc.vector.tensor_copy(out=dst, in_=src)
+            else:
+                nc.scalar.copy(out=dst, in_=src)
+            hi[g, jh, n0] = h_i
 
-        def quant_h(engine, g, jh):
-            codes = one.tile([P, HALF], U32, name="hq%d%d" % (g, jh), align_bytes=64)
-            scales = one.tile([P, HALF], U8, name="hsc%d%d" % (g, jh), align_bytes=64)
-            nc.vector.quantize_mx(out=codes[:].bitcast(F8X4), scales=scales[:], in_=hi[g, jh][:])
-            hq[g, jh], hsc[g, jh] = codes, scales
+        def quant_h(engine, g, jh, n0, width):
+            if (g, jh) not in hq:
+                codes = one.tile([P, HALF], U32, name="hq%d%d" % (g, jh), align_bytes=64)
+                scales = one.tile([P, HALF], U8, name="hsc%d%d" % (g, jh), align_bytes=64)
+                hq[g, jh], hsc[g, jh] = codes, scales
+            cols = slice(n0, n0 + width)
+            nc.vector.quantize_mx(
+                out=hq[g, jh][:, cols].bitcast(F8X4), scales=hsc[g, jh][:, cols], in_=hi[g, jh, n0][:, : 4 * width]
+            )
 
         def stack(engine, j, g):
             if g == 0:
@@ -209,8 +229,10 @@ def tile_seismic_filter_stack_d4_kernel(tc, X_bytes, X_scale, w, gain, v_words, 
 
         def finish(engine, j):
             z = ring.tile([P, R], F32, name="z", bufs=4)
-            nc.vector.tensor_tensor(out=z[:], in0=bank_z[j][:], in1=b_row[:], op=ALU.add)
-            nc.sync.dma_start(out=out[j * P : j * P + P, :], in_=z[:])
+            parts = [(0, R)] if j < 7 else [(0, R // 2), (R // 2, R)]
+            for a, b in parts:
+                nc.vector.tensor_tensor(out=z[:, a:b], in0=bank_z[j][:, a:b], in1=b_row[:, a:b], op=ALU.add)
+                nc.sync.dma_start(out=out[j * P : j * P + P, a:b], in_=z[:, a:b])
 
         def needs(fn, k):
             if fn == turn:
@@ -224,16 +246,14 @@ def tile_seismic_filter_stack_d4_kernel(tc, X_bytes, X_scale, w, gain, v_words, 
             if fn == correlate:
                 qs = range(k[2] // QUART, (k[2] + k[3]) // QUART)
                 return [(quant_x, k[0], c) for c in range(KP)] + [(quant_w, c, q) for c in range(KP) for q in qs]
-            if fn == rectify:
-                return [(signs,)]
             if fn == resign:
                 return [(rectify, k[0], k[1], k[2])]
             if fn == weave_h:
                 return [(resign, s, tt, k[1]) for s in (2 * k[0], 2 * k[0] + 1) for tt in range(2)]
             if fn == quant_h:
-                return [(weave_h, k[0], k[1])]
+                return [(weave_h,) + k]
             if fn == stack:
-                return [(quant_h, k[1], k[0] // 4)]
+                return [(quant_h, k[1], k[0] // 4) + (((0, HALF)) if k[1] < 3 else (k[0] % 4 // 2 * QUART, QUART))]
             if fn == finish:
                 return [(stack, k[0], GROUPS - 1)]
             return []
@@ -243,11 +263,11 @@ def tile_seismic_filter_stack_d4_kernel(tc, X_bytes, X_scale, w, gain, v_words, 
 
         pe, v, sc = [], [], []
         pe += [
-            (turn, 0, 0), (turn, 0, 2), (turn, 0, 1), (turn, 1, 0), (turn, 1, 1), (turn, 1, 2),
-            (correlate, 0, 0, 0, QUART), (correlate, 0, 1, 0, QUART), (correlate, 0, 0, 256, QUART), (correlate, 0, 1, 256, QUART), (correlate, 1, 0, 0, QUART), (correlate, 1, 1, 0, QUART),
-            (correlate, 1, 0, 256, QUART), (correlate, 1, 1, 256, QUART), (correlate, 0, 0, 512, QUART), (correlate, 0, 1, 512, QUART), (correlate, 1, 0, 512, QUART), (correlate, 1, 1, 512, QUART),
-            (turn, 2, 0), (turn, 2, 1), (turn, 2, 2), (correlate, 0, 0, 768, QUART), (correlate, 0, 1, 768, QUART), (correlate, 1, 0, 768, QUART),
-            (correlate, 1, 1, 768, QUART), (turn, 3, 0), (turn, 3, 1), (turn, 3, 2), (correlate, 2, 0, 0, HALF), (correlate, 2, 1, 0, HALF),
+            (turn, 0, 0), (turn, 0, 2), (turn, 0, 1), (turn, 1, 0), (turn, 1, 2), (turn, 1, 1),
+            (correlate, 0, 1, 0, QUART), (correlate, 0, 0, 0, QUART), (correlate, 0, 0, 256, QUART), (correlate, 0, 1, 256, QUART), (turn, 2, 1), (turn, 2, 2),
+            (correlate, 1, 1, 0, QUART), (correlate, 1, 0, 0, QUART), (correlate, 1, 1, 256, QUART), (correlate, 1, 0, 256, QUART), (turn, 2, 0), (correlate, 0, 1, 512, QUART),
+            (correlate, 1, 0, 512, QUART), (correlate, 0, 0, 512, QUART), (correlate, 0, 0, 768, QUART), (correlate, 1, 0, 768, QUART), (correlate, 1, 1, 512, QUART), (correlate, 1, 1, 768, QUART),
+            (correlate, 0, 1, 768, QUART), (turn, 3, 0), (turn, 3, 1), (turn, 3, 2), (correlate, 2, 0, 0, HALF), (correlate, 2, 1, 0, HALF),
             (correlate, 2, 0, 512, HALF), (correlate, 2, 1, 512, HALF), (turn, 4, 0), (turn, 4, 1), (turn, 4, 2), (correlate, 3, 0, 0, HALF),
             (correlate, 3, 1, 0, HALF), (correlate, 3, 0, 512, HALF), (correlate, 3, 1, 512, HALF), (turn, 5, 0), (turn, 5, 1), (turn, 5, 2),
             (correlate, 4, 0, 0, HALF), (correlate, 4, 1, 0, HALF), (correlate, 4, 0, 512, HALF), (correlate, 4, 1, 512, HALF), (turn, 6, 0), (turn, 6, 1),
@@ -256,50 +276,51 @@ def tile_seismic_filter_stack_d4_kernel(tc, X_bytes, X_scale, w, gain, v_words, 
             (correlate, 7, 0, 0, HALF), (correlate, 7, 1, 0, HALF), (correlate, 7, 0, 512, HALF), (correlate, 7, 1, 512, HALF), (stack, 0, 0), (stack, 1, 0),
             (stack, 2, 0), (stack, 3, 0), (stack, 0, 1), (stack, 1, 1), (stack, 2, 1), (stack, 3, 1),
             (stack, 0, 2), (stack, 1, 2), (stack, 2, 2), (stack, 3, 2), (stack, 0, 3), (stack, 1, 3),
-            (stack, 2, 3), (stack, 3, 3), (stack, 4, 0), (stack, 5, 0), (stack, 6, 0), (stack, 7, 0),
-            (stack, 4, 1), (stack, 5, 1), (stack, 6, 1), (stack, 7, 1), (stack, 4, 2), (stack, 5, 2),
-            (stack, 6, 2), (stack, 7, 2), (stack, 4, 3), (stack, 5, 3), (stack, 6, 3), (stack, 7, 3),
+            (stack, 2, 3), (stack, 3, 3), (stack, 4, 0), (stack, 4, 1), (stack, 4, 2), (stack, 4, 3),
+            (stack, 5, 0), (stack, 5, 1), (stack, 5, 2), (stack, 5, 3), (stack, 6, 0), (stack, 6, 1),
+            (stack, 6, 2), (stack, 6, 3), (stack, 7, 0), (stack, 7, 1), (stack, 7, 2), (stack, 7, 3),
         ]
         v += [
-            (widen, 0, 0, 0), (widen, 0, 2, 0), (widen, 0, 1, 0), (widen, 0, 1, 1), (weave_w, 0, 0), (weave_w, 1, 0),
-            (weave_w, 0, 1), (weave_w, 2, 0), (quant_w, 0, 0), (widen, 1, 0, 1), (widen, 1, 2, 1), (quant_w, 1, 0),
-            (weave_w, 2, 1), (quant_w, 0, 1), (signs,), (quant_w, 2, 0), (quant_x, 0, 0), (quant_x, 0, 2),
-            (quant_x, 0, 1), (quant_w, 1, 1), (quant_w, 2, 1), (weave_w, 0, 2), (quant_x, 1, 0), (quant_x, 1, 1),
-            (quant_x, 1, 2), (weave_w, 2, 2), (quant_w, 0, 2), (quant_w, 1, 2), (weave_w, 1, 3), (quant_w, 2, 2),
-            (weave_w, 2, 3), (quant_w, 0, 3), (resign, 0, 0, 0), (widen, 2, 0, 1), (widen, 2, 1, 0), (widen, 2, 1, 1),
-            (quant_w, 1, 3), (resign, 0, 1, 0), (quant_w, 2, 3), (resign, 1, 0, 0), (widen, 3, 0, 1), (widen, 3, 1, 0),
-            (widen, 3, 1, 1), (widen, 3, 2, 0), (widen, 3, 2, 1), (resign, 1, 1, 0), (quant_x, 2, 0), (quant_x, 2, 1),
-            (quant_x, 2, 2), (weave_h, 0, 0), (widen, 4, 0, 0), (widen, 4, 0, 1), (quant_h, 0, 0), (widen, 4, 1, 0),
-            (widen, 4, 2, 0), (resign, 0, 0, 1), (quant_x, 3, 0), (quant_x, 3, 1), (quant_x, 3, 2), (resign, 0, 1, 1),
-            (widen, 5, 0, 0), (widen, 5, 0, 1), (resign, 1, 0, 1), (widen, 5, 1, 1), (widen, 5, 2, 0), (widen, 5, 2, 1),
-            (resign, 1, 1, 1), (resign, 2, 0, 0), (quant_x, 4, 0), (quant_x, 4, 1), (quant_x, 4, 2), (weave_h, 0, 1),
-            (resign, 2, 1, 0), (widen, 6, 0, 0), (widen, 6, 0, 1), (widen, 6, 1, 0), (widen, 6, 1, 1), (quant_h, 0, 1),
-            (widen, 6, 2, 0), (resign, 2, 0, 1), (resign, 2, 1, 1), (resign, 3, 0, 0), (quant_x, 5, 0), (quant_x, 5, 1),
-            (quant_x, 5, 2), (resign, 3, 1, 0), (widen, 7, 0, 0), (widen, 7, 1, 1), (widen, 7, 2, 0), (widen, 7, 2, 1),
-            (resign, 3, 0, 1), (weave_h, 1, 0), (resign, 3, 1, 1), (resign, 4, 0, 0), (quant_x, 6, 0), (quant_x, 6, 1),
-            (quant_x, 6, 2), (quant_h, 1, 0), (weave_h, 1, 1), (resign, 4, 1, 0), (resign, 4, 0, 1), (quant_h, 1, 1),
-            (resign, 4, 1, 1), (resign, 5, 0, 0), (quant_x, 7, 0), (quant_x, 7, 1), (quant_x, 7, 2), (resign, 5, 1, 0),
-            (resign, 5, 0, 1), (weave_h, 2, 0), (resign, 5, 1, 1), (resign, 6, 0, 0), (quant_h, 2, 0), (weave_h, 2, 1),
-            (resign, 6, 1, 0), (resign, 6, 0, 1), (quant_h, 2, 1), (resign, 6, 1, 1), (resign, 7, 0, 0), (resign, 7, 1, 0),
-            (resign, 7, 0, 1), (weave_h, 3, 0), (resign, 7, 1, 1), (quant_h, 3, 0), (weave_h, 3, 1), (quant_h, 3, 1),
-            (finish, 0), (finish, 1), (finish, 2), (finish, 3), (finish, 4), (finish, 5),
-            (finish, 6), (finish, 7),
+            (widen, 0, 0, 1), (widen, 0, 1, 1), (widen, 0, 2, 1), (widen, 0, 2, 0), (widen, 0, 1, 0), (weave_w, 0, 0),
+            (quant_x, 0, 0), (quant_w, 0, 0), (weave_w, 1, 1), (quant_w, 0, 1), (quant_w, 1, 1), (weave_w, 2, 0),
+            (quant_x, 0, 2), (widen, 1, 1, 1), (weave_w, 2, 1), (widen, 1, 0, 0), (quant_w, 2, 0), (quant_w, 2, 1),
+            (quant_w, 1, 0), (quant_x, 0, 1), (weave_w, 1, 2), (quant_x, 1, 0), (weave_w, 2, 2), (quant_x, 1, 2),
+            (widen, 2, 1, 1), (widen, 2, 2, 0), (widen, 2, 2, 1), (quant_x, 1, 1), (widen, 2, 0, 1), (quant_w, 1, 2),
+            (weave_w, 2, 3), (quant_w, 0, 2), (quant_w, 2, 3), (quant_w, 2, 2), (weave_w, 0, 3), (quant_w, 1, 3),
+            (quant_w, 0, 3), (widen, 3, 1, 0), (widen, 3, 0, 1), (quant_x, 2, 2), (widen, 3, 1, 1), (quant_x, 2, 0),
+            (widen, 3, 0, 0), (widen, 3, 2, 0), (widen, 3, 2, 1), (quant_x, 2, 1), (resign, 1, 0, 0), (widen, 4, 0, 0),
+            (collect, 3, 1), (widen, 5, 2, 0), (widen, 4, 2, 0), (resign, 0, 0, 0), (widen, 4, 1, 1), (quant_x, 3, 1),
+            (resign, 0, 0, 1), (widen, 4, 1, 0), (widen, 4, 2, 1), (resign, 1, 1, 0), (quant_x, 3, 0), (resign, 0, 1, 0),
+            (quant_x, 3, 2), (weave_h, 0, 0, 0, HALF), (resign, 1, 1, 1), (quant_h, 0, 0, 0, HALF), (widen, 5, 0, 0), (resign, 0, 1, 1),
+            (resign, 1, 0, 1), (widen, 5, 1, 1), (widen, 5, 2, 1), (resign, 2, 0, 0), (quant_x, 4, 0), (quant_x, 4, 1),
+            (quant_x, 4, 2), (weave_h, 0, 1, 0, HALF), (resign, 2, 1, 0), (widen, 6, 0, 1), (widen, 6, 1, 0), (widen, 6, 2, 0),
+            (widen, 6, 2, 1), (resign, 2, 0, 1), (quant_h, 0, 1, 0, HALF), (resign, 2, 1, 1), (resign, 3, 0, 0), (quant_x, 5, 0),
+            (quant_x, 5, 1), (quant_x, 5, 2), (resign, 3, 1, 0), (widen, 7, 0, 0), (widen, 7, 0, 1), (widen, 7, 1, 0),
+            (widen, 7, 1, 1), (resign, 3, 0, 1), (weave_h, 1, 0, 0, HALF), (resign, 3, 1, 1), (resign, 4, 0, 0), (quant_x, 6, 0),
+            (quant_x, 6, 1), (quant_x, 6, 2), (quant_h, 1, 0, 0, HALF), (weave_h, 1, 1, 0, HALF), (resign, 4, 1, 0), (resign, 4, 0, 1),
+            (quant_h, 1, 1, 0, HALF), (resign, 4, 1, 1), (resign, 5, 0, 0), (quant_x, 7, 0), (quant_x, 7, 1), (quant_x, 7, 2),
+            (resign, 5, 1, 0), (resign, 5, 0, 1), (weave_h, 2, 0, 0, HALF), (resign, 5, 1, 1), (resign, 6, 0, 0), (quant_h, 2, 0, 0, HALF),
+            (weave_h, 2, 1, 0, HALF), (resign, 6, 1, 0), (resign, 6, 0, 1), (quant_h, 2, 1, 0, HALF), (resign, 6, 1, 1), (resign, 7, 0, 0),
+            (resign, 7, 1, 0), (resign, 7, 0, 1), (resign, 7, 1, 1), (weave_h, 3, 0, 0, QUART), (quant_h, 3, 0, 0, QUART), (quant_h, 3, 0, 256, QUART),
+            (weave_h, 3, 1, 0, QUART), (quant_h, 3, 1, 0, QUART), (finish, 0), (quant_h, 3, 1, 256, QUART), (finish, 1), (finish, 2),
+            (finish, 3), (finish, 4), (finish, 5), (finish, 6), (finish, 7),
         ]
         sc += [
-            (widen, 0, 0, 1), (widen, 0, 2, 1), (collect, 0, 0), (collect, 0, 2), (collect, 0, 1), (weave_w, 1, 1),
-            (widen, 1, 0, 0), (widen, 1, 1, 0), (widen, 1, 1, 1), (widen, 1, 2, 0), (collect, 1, 0), (collect, 1, 1),
-            (collect, 1, 2), (weave_w, 1, 2), (rectify, 0, 0, 0), (weave_w, 0, 3), (rectify, 0, 1, 0), (rectify, 1, 0, 0),
-            (widen, 2, 0, 0), (widen, 2, 2, 0), (widen, 2, 2, 1), (rectify, 1, 1, 0), (collect, 2, 0), (collect, 2, 1),
-            (collect, 2, 2), (widen, 3, 0, 0), (rectify, 0, 0, 1), (rectify, 0, 1, 1), (collect, 3, 0), (collect, 3, 1),
-            (collect, 3, 2), (rectify, 1, 0, 1), (widen, 4, 1, 1), (widen, 4, 2, 1), (rectify, 1, 1, 1), (rectify, 2, 0, 0),
-            (collect, 4, 0), (collect, 4, 1), (collect, 4, 2), (rectify, 2, 1, 0), (widen, 5, 1, 0), (rectify, 2, 0, 1),
-            (rectify, 2, 1, 1), (rectify, 3, 0, 0), (collect, 5, 0), (collect, 5, 1), (collect, 5, 2), (rectify, 3, 1, 0),
-            (widen, 6, 2, 1), (rectify, 3, 0, 1), (rectify, 3, 1, 1), (rectify, 4, 0, 0), (collect, 6, 0), (collect, 6, 1),
-            (collect, 6, 2), (rectify, 4, 1, 0), (widen, 7, 0, 1), (widen, 7, 1, 0), (rectify, 4, 0, 1), (rectify, 4, 1, 1),
-            (rectify, 5, 0, 0), (collect, 7, 0), (collect, 7, 1), (collect, 7, 2), (rectify, 5, 1, 0), (rectify, 5, 0, 1),
-            (rectify, 5, 1, 1), (rectify, 6, 0, 0), (rectify, 6, 1, 0), (rectify, 6, 0, 1), (rectify, 6, 1, 1), (rectify, 7, 0, 0),
-            (rectify, 7, 1, 0), (rectify, 7, 0, 1), (rectify, 7, 1, 1),
+            (widen, 0, 0, 0), (collect, 0, 0), (weave_w, 0, 1), (collect, 0, 1), (collect, 0, 2), (weave_w, 1, 0),
+            (widen, 1, 2, 1), (widen, 1, 0, 1), (widen, 1, 2, 0), (widen, 1, 1, 0), (collect, 1, 0), (collect, 1, 2),
+            (collect, 1, 1), (widen, 2, 1, 0), (widen, 2, 0, 0), (weave_w, 0, 2), (collect, 2, 2), (weave_w, 1, 3),
+            (collect, 2, 0), (rectify, 1, 0, 0), (rectify, 0, 1, 0), (collect, 2, 1), (rectify, 0, 0, 1), (rectify, 1, 1, 0),
+            (rectify, 0, 0, 0), (rectify, 1, 1, 1), (widen, 4, 0, 1), (collect, 3, 0), (widen, 5, 0, 1), (rectify, 0, 1, 1),
+            (collect, 3, 2), (rectify, 1, 0, 1), (rectify, 2, 0, 0), (collect, 4, 0), (collect, 4, 1), (collect, 4, 2),
+            (rectify, 2, 1, 0), (widen, 5, 1, 0), (rectify, 2, 0, 1), (rectify, 2, 1, 1), (rectify, 3, 0, 0), (collect, 5, 0),
+            (collect, 5, 1), (collect, 5, 2), (rectify, 3, 1, 0), (widen, 6, 0, 0), (widen, 6, 1, 1), (rectify, 3, 0, 1),
+            (rectify, 3, 1, 1), (rectify, 4, 0, 0), (collect, 6, 0), (collect, 6, 1), (collect, 6, 2), (rectify, 4, 1, 0),
+            (widen, 7, 2, 0), (widen, 7, 2, 1), (rectify, 4, 0, 1), (rectify, 4, 1, 1), (rectify, 5, 0, 0), (collect, 7, 0),
+            (collect, 7, 1), (collect, 7, 2), (rectify, 5, 1, 0), (rectify, 5, 0, 1), (rectify, 5, 1, 1), (rectify, 6, 0, 0),
+            (rectify, 6, 1, 0), (rectify, 6, 0, 1), (rectify, 6, 1, 1), (rectify, 7, 0, 0), (rectify, 7, 1, 0), (rectify, 7, 0, 1),
+            (rectify, 7, 1, 1), (weave_h, 3, 0, 256, QUART), (weave_h, 3, 1, 256, QUART),
         ]
+        signs("g")
         queues = {"p": pe, "v": v, "s": sc}
         at = {"p": 0, "v": 0, "s": 0}
         issued = set()

from contextlib import ExitStack

import concourse.mybir as mybir
from concourse.masks import make_identity

M, K, N, R = 2048, 1536, 1024, 512
FLOPS = 2 * M * K * N + 2 * N * M * R

F32 = mybir.dt.float32
BF16 = mybir.dt.bfloat16
I32 = mybir.dt.int32
U32 = mybir.dt.uint32
U8 = mybir.dt.uint8
F8 = mybir.dt.float8_e4m3fn
F8X4 = mybir.dt.float8_e4m3fn_x4
F4X4 = mybir.dt.float4_e2m1fn_x4
ALU = mybir.AluOpType
ACT = mybir.ActivationFunctionType

P = 128
PASS = 512
KP = K // PASS
GROUPS = M // PASS
STEPS = 2 * GROUPS
HALF = 512
X_PARTS = [(0, 512), (512, 1024), (1024, 1536)]
QUART = 256


def tile_seismic_filter_stack_d4_kernel(tc, X_bytes, X_scale, w, gain, v_words, v_scales, bias, out):
    nc = tc.nc
    x_rows = X_bytes.rearrange("(g p t) k -> g p t k", p=P, t=4)
    w_rows = w.rearrange("(c p t) n -> c p t n", p=P, t=4)

    with ExitStack() as ctx:
        one = ctx.enter_context(tc.tile_pool(name="one", bufs=1))
        ring = ctx.enter_context(tc.tile_pool(name="ring", bufs=3))
        psum = ctx.enter_context(tc.psum_pool(name="psum", bufs=8))
        ctx.enter_context(tc.manual_schedule())

        ident = one.tile([P, P], F32, name="ident")
        make_identity(nc, ident[:])
        v_sc = one.tile([P, GROUPS, R], U8, name="v_sc", align_bytes=64)
        nc.gpsimd.memset(v_sc[:].rearrange("p g r -> p (g r)").bitcast(I32), 0)

        minus = one.tile([P, 1], F32, name="minus")
        unit = one.tile([P, 1], F32, name="unit")
        nc.vector.memset(minus[:], -1.0)
        nc.scalar.activation(out=unit[:], in_=minus[:], func=ACT.Abs)

        xs = one.tile([P, GROUPS, 48], F32, name="xs")
        x_scale = X_scale.rearrange("(g p t) c -> p g (t c)", p=P, t=4)
        nc.sync.dma_start(out=xs[:, 0, :], in_=x_scale[:, 0, :])
        xb = {}

        def load_x(s):
            rows = x_rows[s // 2][:, 2 * (s % 2) : 2 * (s % 2) + 2, :]
            for a, b in X_PARTS if s == 0 else [(0, K)]:
                x_b = one.tile([P, 2, b - a], U8, name="x_bytes%d_%d" % (s, a))
                nc.sync.dma_start(out=x_b[:], in_=rows[:, :, a:b])
                for k in range(a, b, P):
                    xb[s, k] = x_b[:, :, k - a : k - a + P]

        wr = {}

        def load_w(jh, c):
            w_raw = one.tile([P, 4, HALF], BF16, name="w_raw%d%d" % (jh, c))
            nc.sync.dma_start(out=w_raw[:], in_=w_rows[c][:, :, jh * HALF : (jh + 1) * HALF])
            wr[jh, c] = w_raw

        load_x(0)
        for c in range(KP):
            load_w(0, c)
        load_x(1)
        nc.sync.dma_start(out=xs[:, 1:, :], in_=x_scale[:, 1:, :])
        g_raw = one.tile([P, GROUPS, 4], BF16, name="g_raw")
        nc.sync.dma_start(out=g_raw[:], in_=gain.rearrange("(g p t) -> p g t", p=P, t=4))
        for c in range(KP):
            load_w(1, c)
        for s in range(2, STEPS):
            load_x(s)
        v_w = one.tile([P, GROUPS, 2 * R], U8, name="v_w", align_bytes=64)
        for g in range(GROUPS):
            nc.sync.dma_start(out=v_w[:, g, :].bitcast(I32), in_=v_words[g].bitcast(I32))
        for q in range(4):
            nc.sync.dma_start(
                out=v_sc[32 * q : 32 * q + 4, :, :].bitcast(I32),
                in_=v_scales[:, 4 * q : 4 * q + 4, :].rearrange("g q r -> q g r").bitcast(I32),
            )
        b_row = one.tile([P, R], BF16, name="b_row")
        nc.sync.dma_start(out=b_row[:], in_=bias.partition_broadcast(P))

        gain_f = one.tile([P, GROUPS * 4], F32, name="gain_f")
        sign_f = one.tile([P, GROUPS * 4], F32, name="sign_f")
        wq = [one.tile([P, N], U32, name="wq%d" % c, align_bytes=64) for c in range(KP)]
        wsc = [one.tile([P, N], U8, name="wsc%d" % c, align_bytes=64) for c in range(KP)]
        xw, by_pairs, xi, xq, xsc, wi, hp, hi, hq, hsc, bank_x, bank_c, bank_z = [{} for i in range(13)]

        def widen(engine, s, c, tt):
            g, t = s // 2, 2 * (s % 2) + tt
            if (s, c) not in xw:
                x_w = ring.tile([P, 2, PASS], BF16, name="x_w", bufs=12)
                xw[s, c] = x_w
            by_pairs[s, c, tt] = engine == "v"
            for q in range(4):
                k0 = c * PASS + q * P
                src = xb[s, k0][:, tt, :].bitcast(F8)
                scale = xs[:, g, t * 12 + c * 4 + q : t * 12 + c * 4 + q + 1]
                if engine == "v":
                    dst = xw[s, c][:, tt, :].rearrange("p (u k e) -> p k u e", u=2, e=2)[:, 32 * q : 32 * q + 32, :, :]
                    nc.vector.tensor_scalar(
                        out=dst, in0=src.rearrange("p (k u e) -> p k u e", u=2, e=2), scalar1=scale, scalar2=None, op0=ALU.mult
                    )
                else:
                    nc.scalar.activation(out=xw[s, c][:, tt, q * P : q * P + P], in_=src, func=ACT.Copy, scale=scale)

        def turn(engine, s, c):
            bank = psum.tile([P, 512], F32, name="bank")
            for tt in range(2):
                words = xw[s, c][:, tt, :].bitcast(F32)
                for u in range(2):
                    pick = words[:, u * P : u * P + P] if by_pairs[s, c, tt] else words[:, u : 2 * P : 2]
                    j = 2 * tt + u
                    nc.tensor.transpose(bank[:, j * P : j * P + P], pick, ident[:])
            bank_x[s, c] = bank

        def collect(engine, s, c):
            x_i = ring.tile([P, 2 * P * 4], BF16, name="x_i", align_bytes=64, bufs=6)
            dst = x_i[:].bitcast(F32).rearrange("p (a m u) -> p a m u", a=2, u=2)
            src = bank_x[s, c][:].rearrange("p (a u m) -> p a m u", a=2, u=2)
            if engine == "v":
                nc.vector.tensor_copy(out=dst, in_=src)
            else:
                nc.scalar.copy(out=dst, in_=src)
            xi[s, c] = x_i

        def quant_x(engine, s, c):
            codes = one.tile([P, 2 * P], U32, name="xq%d%d" % (s, c), align_bytes=64)
            scales = one.tile([P, 2 * P], U8, name="xsc%d%d" % (s, c), align_bytes=64)
            nc.vector.quantize_mx(out=codes[:].bitcast(F8X4), scales=scales[:], in_=xi[s, c][:])
            xq[s, c], xsc[s, c] = codes, scales

        def weave_w(engine, c, q):
            w_i = ring.tile([P, QUART * 4], BF16, name="w_i", align_bytes=64, bufs=6)
            cols = slice(q % 2 * QUART, q % 2 * QUART + QUART)
            dst = w_i[:].rearrange("p (n i t) -> p n t i", i=4, t=4)
            src = wr[q // 2, c][:, :, cols].rearrange("p t (n i) -> p n t i", i=4)
            if engine == "v":
                nc.vector.tensor_copy(out=dst, in_=src)
            else:
                nc.scalar.copy(out=dst, in_=src)
            wi[c, q] = w_i

        def quant_w(engine, c, q):
            cols = slice(q * QUART, q * QUART + QUART)
            nc.vector.quantize_mx(out=wq[c][:, cols].bitcast(F8X4), scales=wsc[c][:, cols], in_=wi[c, q][:])

        def signs(engine):
            nc.gpsimd.tensor_copy(out=gain_f[:], in_=g_raw[:].rearrange("p g t -> p (g t)"))
            nc.gpsimd.tensor_scalar(out=sign_f[:], in0=gain_f[:], scalar1=0.0, scalar2=2.0, op0=ALU.is_ge, op1=ALU.mult)
            nc.gpsimd.tensor_scalar(out=sign_f[:], in0=sign_f[:], scalar1=unit[:], scalar2=None, op0=ALU.subtract)

        def correlate(engine, s, tt, n0, width):
            jh = n0 // HALF
            if n0 % HALF == 0:
                bank = psum.tile([P, 512], F32, name="bank")
                bank_c[s, tt, jh] = bank
            rows = slice(tt * P, tt * P + P)
            cols = slice(n0, n0 + width)
            for c in range(KP):
                nc.tensor.matmul_mx(
                    out=bank_c[s, tt, jh][:, n0 % HALF : n0 % HALF + width],
                    lhsT=xq[s, c][:, rows].bitcast(F8X4),
                    lhsT_scale=xsc[s, c][:, rows],
                    rhs=wq[c][:, cols].bitcast(F8X4),
                    rhs_scale=wsc[c][:, cols],
                    start=(c == 0),
                    stop=(c == KP - 1),
                )

        def rectify(engine, s, tt, jh):
            g, t = s // 2, 2 * (s % 2) + tt
            if (g, jh) not in hp:
                h_p = ring.tile([P, 4, HALF], BF16, name="h_p", bufs=4)
                hp[g, jh] = h_p
            nc.scalar.activation(
                out=hp[g, jh][:, t, :], in_=bank_c[s, tt, jh][:], func=ACT.Abs, scale=gain_f[:, 4 * g + t : 4 * g + t + 1]
            )

        def resign(engine, s, tt, jh):
            g, t = s // 2, 2 * (s % 2) + tt
            h = hp[g, jh][:, t, :]
            nc.vector.tensor_scalar(out=h, in0=h, scalar1=sign_f[:, 4 * g + t : 4 * g + t + 1], scalar2=None, op0=ALU.mult)

        def weave_h(engine, g, jh, n0, width):
            h_i = ring.tile([P, HALF * 4], BF16, name="h_i", align_bytes=64, bufs=4)
            dst = h_i[:, : 4 * width].rearrange("p (n i t) -> p n t i", i=4, t=4)
            src = hp[g, jh][:, :, n0 : n0 + width].rearrange("p t (n i) -> p n t i", i=4)
            if engine == "v":
                nc.vector.tensor_copy(out=dst, in_=src)
            else:
                nc.scalar.copy(out=dst, in_=src)
            hi[g, jh, n0] = h_i

        def quant_h(engine, g, jh, n0, width):
            if (g, jh) not in hq:
                codes = one.tile([P, HALF], U32, name="hq%d%d" % (g, jh), align_bytes=64)
                scales = one.tile([P, HALF], U8, name="hsc%d%d" % (g, jh), align_bytes=64)
                hq[g, jh], hsc[g, jh] = codes, scales
            cols = slice(n0, n0 + width)
            nc.vector.quantize_mx(
                out=hq[g, jh][:, cols].bitcast(F8X4), scales=hsc[g, jh][:, cols], in_=hi[g, jh, n0][:, : 4 * width]
            )

        def stack(engine, j, g):
            if g == 0:
                bank = psum.tile([P, 512], F32, name="bank")
                bank_z[j] = bank
            cols = slice(j % 4 * P, j % 4 * P + P)
            nc.tensor.matmul_mx(
                out=bank_z[j][:],
                lhsT=hq[g, j // 4][:, cols].bitcast(F8X4),
                lhsT_scale=hsc[g, j // 4][:, cols],
                rhs=v_w[:, g, :].bitcast(F4X4),
                rhs_scale=v_sc[:, g, :],
                start=(g == 0),
                stop=(g == GROUPS - 1),
            )

        def finish(engine, j):
            z = ring.tile([P, R], F32, name="z", bufs=4)
            parts = [(0, R)] if j < 7 else [(0, R // 2), (R // 2, R)]
            for a, b in parts:
                nc.vector.tensor_tensor(out=z[:, a:b], in0=bank_z[j][:, a:b], in1=b_row[:, a:b], op=ALU.add)
                nc.sync.dma_start(out=out[j * P : j * P + P, a:b], in_=z[:, a:b])

        def needs(fn, k):
            if fn == turn:
                return [(widen, k[0], k[1], tt) for tt in range(2)]
            if fn == collect:
                return [(turn, k[0], k[1])]
            if fn == quant_x:
                return [(collect, k[0], k[1])]
            if fn == quant_w:
                return [(weave_w, k[0], k[1])]
            if fn == correlate:
                qs = range(k[2] // QUART, (k[2] + k[3]) // QUART)
                return [(quant_x, k[0], c) for c in range(KP)] + [(quant_w, c, q) for c in range(KP) for q in qs]
            if fn == resign:
                return [(rectify, k[0], k[1], k[2])]
            if fn == weave_h:
                return [(resign, s, tt, k[1]) for s in (2 * k[0], 2 * k[0] + 1) for tt in range(2)]
            if fn == quant_h:
                return [(weave_h,) + k]
            if fn == stack:
                return [(quant_h, k[1], k[0] // 4) + (((0, HALF)) if k[1] < 3 else (k[0] % 4 // 2 * QUART, QUART))]
            if fn == finish:
                return [(stack, k[0], GROUPS - 1)]
            return []

        def quarters(s, tt, jh):
            return [(correlate, s, tt, jh * HALF + i * QUART, QUART) for i in range(2)]

        pe, v, sc = [], [], []
        pe += [
            (turn, 0, 0), (turn, 0, 2), (turn, 0, 1), (turn, 1, 0), (turn, 1, 2), (turn, 1, 1),
            (correlate, 0, 1, 0, QUART), (correlate, 0, 0, 0, QUART), (correlate, 0, 0, 256, QUART), (correlate, 0, 1, 256, QUART), (turn, 2, 1), (turn, 2, 2),
            (correlate, 1, 1, 0, QUART), (correlate, 1, 0, 0, QUART), (correlate, 1, 1, 256, QUART), (correlate, 1, 0, 256, QUART), (turn, 2, 0), (correlate, 0, 1, 512, QUART),
            (correlate, 1, 0, 512, QUART), (correlate, 0, 0, 512, QUART), (correlate, 0, 0, 768, QUART), (correlate, 1, 0, 768, QUART), (correlate, 1, 1, 512, QUART), (correlate, 1, 1, 768, QUART),
            (correlate, 0, 1, 768, QUART), (turn, 3, 0), (turn, 3, 1), (turn, 3, 2), (correlate, 2, 0, 0, HALF), (correlate, 2, 1, 0, HALF),
            (correlate, 2, 0, 512, HALF), (correlate, 2, 1, 512, HALF), (turn, 4, 0), (turn, 4, 1), (turn, 4, 2), (correlate, 3, 0, 0, HALF),
            (correlate, 3, 1, 0, HALF), (correlate, 3, 0, 512, HALF), (correlate, 3, 1, 512, HALF), (turn, 5, 0), (turn, 5, 1), (turn, 5, 2),
            (correlate, 4, 0, 0, HALF), (correlate, 4, 1, 0, HALF), (correlate, 4, 0, 512, HALF), (correlate, 4, 1, 512, HALF), (turn, 6, 0), (turn, 6, 1),
            (turn, 6, 2), (correlate, 5, 0, 0, HALF), (correlate, 5, 1, 0, HALF), (correlate, 5, 0, 512, HALF), (correlate, 5, 1, 512, HALF), (turn, 7, 0),
            (turn, 7, 1), (turn, 7, 2), (correlate, 6, 0, 0, HALF), (correlate, 6, 1, 0, HALF), (correlate, 6, 0, 512, HALF), (correlate, 6, 1, 512, HALF),
            (correlate, 7, 0, 0, HALF), (correlate, 7, 1, 0, HALF), (correlate, 7, 0, 512, HALF), (correlate, 7, 1, 512, HALF), (stack, 0, 0), (stack, 1, 0),
            (stack, 2, 0), (stack, 3, 0), (stack, 0, 1), (stack, 1, 1), (stack, 2, 1), (stack, 3, 1),
            (stack, 0, 2), (stack, 1, 2), (stack, 2, 2), (stack, 3, 2), (stack, 0, 3), (stack, 1, 3),
            (stack, 2, 3), (stack, 3, 3), (stack, 4, 0), (stack, 4, 1), (stack, 4, 2), (stack, 4, 3),
            (stack, 5, 0), (stack, 5, 1), (stack, 5, 2), (stack, 5, 3), (stack, 6, 0), (stack, 6, 1),
            (stack, 6, 2), (stack, 6, 3), (stack, 7, 0), (stack, 7, 1), (stack, 7, 2), (stack, 7, 3),
        ]
        v += [
            (widen, 0, 0, 1), (widen, 0, 1, 1), (widen, 0, 2, 1), (widen, 0, 2, 0), (widen, 0, 1, 0), (weave_w, 0, 0),
            (quant_x, 0, 0), (quant_w, 0, 0), (weave_w, 1, 1), (quant_w, 0, 1), (quant_w, 1, 1), (weave_w, 2, 0),
            (quant_x, 0, 2), (widen, 1, 1, 1), (weave_w, 2, 1), (widen, 1, 0, 0), (quant_w, 2, 0), (quant_w, 2, 1),
            (quant_w, 1, 0), (quant_x, 0, 1), (weave_w, 1, 2), (quant_x, 1, 0), (weave_w, 2, 2), (quant_x, 1, 2),
            (widen, 2, 1, 1), (widen, 2, 2, 0), (widen, 2, 2, 1), (quant_x, 1, 1), (widen, 2, 0, 1), (quant_w, 1, 2),
            (weave_w, 2, 3), (quant_w, 0, 2), (quant_w, 2, 3), (quant_w, 2, 2), (weave_w, 0, 3), (quant_w, 1, 3),
            (quant_w, 0, 3), (widen, 3, 1, 0), (widen, 3, 0, 1), (quant_x, 2, 2), (widen, 3, 1, 1), (quant_x, 2, 0),
            (widen, 3, 0, 0), (widen, 3, 2, 0), (widen, 3, 2, 1), (quant_x, 2, 1), (resign, 1, 0, 0), (widen, 4, 0, 0),
            (collect, 3, 1), (widen, 5, 2, 0), (widen, 4, 2, 0), (resign, 0, 0, 0), (widen, 4, 1, 1), (quant_x, 3, 1),
            (resign, 0, 0, 1), (widen, 4, 1, 0), (widen, 4, 2, 1), (resign, 1, 1, 0), (quant_x, 3, 0), (resign, 0, 1, 0),
            (quant_x, 3, 2), (weave_h, 0, 0, 0, HALF), (resign, 1, 1, 1), (quant_h, 0, 0, 0, HALF), (widen, 5, 0, 0), (resign, 0, 1, 1),
            (resign, 1, 0, 1), (widen, 5, 1, 1), (widen, 5, 2, 1), (resign, 2, 0, 0), (quant_x, 4, 0), (quant_x, 4, 1),
            (quant_x, 4, 2), (weave_h, 0, 1, 0, HALF), (resign, 2, 1, 0), (widen, 6, 0, 1), (widen, 6, 1, 0), (widen, 6, 2, 0),
            (widen, 6, 2, 1), (resign, 2, 0, 1), (quant_h, 0, 1, 0, HALF), (resign, 2, 1, 1), (resign, 3, 0, 0), (quant_x, 5, 0),
            (quant_x, 5, 1), (quant_x, 5, 2), (resign, 3, 1, 0), (widen, 7, 0, 0), (widen, 7, 0, 1), (widen, 7, 1, 0),
            (widen, 7, 1, 1), (resign, 3, 0, 1), (weave_h, 1, 0, 0, HALF), (resign, 3, 1, 1), (resign, 4, 0, 0), (quant_x, 6, 0),
            (quant_x, 6, 1), (quant_x, 6, 2), (quant_h, 1, 0, 0, HALF), (weave_h, 1, 1, 0, HALF), (resign, 4, 1, 0), (resign, 4, 0, 1),
            (quant_h, 1, 1, 0, HALF), (resign, 4, 1, 1), (resign, 5, 0, 0), (quant_x, 7, 0), (quant_x, 7, 1), (quant_x, 7, 2),
            (resign, 5, 1, 0), (resign, 5, 0, 1), (weave_h, 2, 0, 0, HALF), (resign, 5, 1, 1), (resign, 6, 0, 0), (quant_h, 2, 0, 0, HALF),
            (weave_h, 2, 1, 0, HALF), (resign, 6, 1, 0), (resign, 6, 0, 1), (quant_h, 2, 1, 0, HALF), (resign, 6, 1, 1), (resign, 7, 0, 0),
            (resign, 7, 1, 0), (resign, 7, 0, 1), (resign, 7, 1, 1), (weave_h, 3, 0, 0, QUART), (quant_h, 3, 0, 0, QUART), (quant_h, 3, 0, 256, QUART),
            (weave_h, 3, 1, 0, QUART), (quant_h, 3, 1, 0, QUART), (finish, 0), (quant_h, 3, 1, 256, QUART), (finish, 1), (finish, 2),
            (finish, 3), (finish, 4), (finish, 5), (finish, 6), (finish, 7),
        ]
        sc += [
            (widen, 0, 0, 0), (collect, 0, 0), (weave_w, 0, 1), (collect, 0, 1), (collect, 0, 2), (weave_w, 1, 0),
            (widen, 1, 2, 1), (widen, 1, 0, 1), (widen, 1, 2, 0), (widen, 1, 1, 0), (collect, 1, 0), (collect, 1, 2),
            (collect, 1, 1), (widen, 2, 1, 0), (widen, 2, 0, 0), (weave_w, 0, 2), (collect, 2, 2), (weave_w, 1, 3),
            (collect, 2, 0), (rectify, 1, 0, 0), (rectify, 0, 1, 0), (collect, 2, 1), (rectify, 0, 0, 1), (rectify, 1, 1, 0),
            (rectify, 0, 0, 0), (rectify, 1, 1, 1), (widen, 4, 0, 1), (collect, 3, 0), (widen, 5, 0, 1), (rectify, 0, 1, 1),
            (collect, 3, 2), (rectify, 1, 0, 1), (rectify, 2, 0, 0), (collect, 4, 0), (collect, 4, 1), (collect, 4, 2),
            (rectify, 2, 1, 0), (widen, 5, 1, 0), (rectify, 2, 0, 1), (rectify, 2, 1, 1), (rectify, 3, 0, 0), (collect, 5, 0),
            (collect, 5, 1), (collect, 5, 2), (rectify, 3, 1, 0), (widen, 6, 0, 0), (widen, 6, 1, 1), (rectify, 3, 0, 1),
            (rectify, 3, 1, 1), (rectify, 4, 0, 0), (collect, 6, 0), (collect, 6, 1), (collect, 6, 2), (rectify, 4, 1, 0),
            (widen, 7, 2, 0), (widen, 7, 2, 1), (rectify, 4, 0, 1), (rectify, 4, 1, 1), (rectify, 5, 0, 0), (collect, 7, 0),
            (collect, 7, 1), (collect, 7, 2), (rectify, 5, 1, 0), (rectify, 5, 0, 1), (rectify, 5, 1, 1), (rectify, 6, 0, 0),
            (rectify, 6, 1, 0), (rectify, 6, 0, 1), (rectify, 6, 1, 1), (rectify, 7, 0, 0), (rectify, 7, 1, 0), (rectify, 7, 0, 1),
            (rectify, 7, 1, 1), (weave_h, 3, 0, 256, QUART), (weave_h, 3, 1, 256, QUART),
        ]
        signs("g")
        queues = {"p": pe, "v": v, "s": sc}
        at = {"p": 0, "v": 0, "s": 0}
        issued = set()
        halves = {}
        while any(at[e] < len(queues[e]) for e in queues):
            moved = False
            for e in queues:
                while at[e] < len(queues[e]):
                    fn, key = queues[e][at[e]][0], queues[e][at[e]][1:]
                    need = needs(fn, key)
                    if fn == rectify:
                        need = need + [("corr",) + key]
                    if any(n not in issued for n in need):
                        break
                    fn(e, *key)
                    issued.add((fn,) + key)
                    if fn == correlate:
                        w = halves.get((key[0], key[1], key[2] // HALF), 0) + key[3]
                        halves[key[0], key[1], key[2] // HALF] = w
                        if w == HALF:
                            issued.add(("corr", key[0], key[1], key[2] // HALF))
                    at[e] += 1
                    moved = True
            assert moved
